import numpy as np, ml_dtypes
CORES = [66,74,82,90,194,202,210,218]
N = 8
BF = ml_dtypes.bfloat16
def gentries(a):
    return np.ascontiguousarray(a.reshape(8, 16, -1).transpose(0, 2, 1)).reshape(8, -1)
def gtable(e):
    e = np.asarray(e); return np.ascontiguousarray(e.reshape(8, -1, 16).transpose(0, 2, 1)).reshape(128, -1).astype(np.int32)
K, D, SH = 256, 4096, 2
def sized(rng):
    return rng.standard_normal((N, 128, D), dtype=np.float32) * np.exp2(rng.integers(-1, 2, (N, 128, 1))).astype(np.float32)
def hashes(a, b):
    return np.repeat(np.stack([a, b], 2), 16, axis=1).astype(np.int32)
def lists(e):
    return np.stack([gtable(u) for u in e])
def setup_inputs(rng):
    a = np.stack([rng.permutation(255)[:8] + 1 for r in range(N)]); b = rng.integers(0, 65536, (N, 8))
    return {"mat": sized(rng).astype(BF), "ids": lists(rng.integers(0, 65536, (N, 8, K))), "hs": hashes(a, b)}
def setup_inputs_ends(rng):
    e = rng.integers(0, 65536, (N, 8, K)); e = np.where(rng.random(e.shape) < 0.5, rng.choice(np.array([0, 1, 65534, 65535]), e.shape), e)
    e[:, :, 0] = 0; e[:, :, 1] = 1 << SH; e[:, :, -1] = 65535
    top = (D - 1) << SH; low = (1 << SH) - 1
    a = rng.choice(np.array([0, 1, 254, 255]), (N, 8)); b = rng.choice(np.array([0, 1, low, top, top + low, 65535]), (N, 8))
    for r in range(N):
        a[r, r % 8], b[r, r % 8] = 1, top
        a[r, (r + 1) % 8], b[r, (r + 1) % 8] = 255, 65535
        a[r, (r + 2) % 8] = 0
        a[r, (r + 3) % 8], b[r, (r + 3) % 8] = 1, top + low
    return {"mat": sized(rng).astype(BF), "ids": lists(e), "hs": hashes(a, b)}
def setup_inputs_one(rng):
    d = setup_inputs(rng); e = rng.integers(0, 65536, (N, 8, K)); o = rng.permutation(N)
    e[o[0]] = rng.permutation(65536)[:8, None]; e[o[1]] = e[o[2]]; e[o[3]] = np.repeat(e[o[3], :, :K // 16], 16, axis=1)
    d["ids"] = lists(e); d["hs"][rng.integers(0, N), :, 0] = 0; return d
def setup_inputs_turns(rng):
    d = setup_inputs(rng); p = np.argsort(rng.random((N, 8, D, 4)), axis=3)
    w = (rng.integers(128, 256, p.shape) * (2 * rng.integers(0, 2, p.shape) - 1)).astype(np.float32) * np.float32(2.0 ** -7)
    m = np.where(p[..., None] == np.arange(4), w[..., None], np.float32(0))
    d["mat"] = np.ascontiguousarray(m.transpose(0, 1, 3, 4, 2)).reshape(N, 128, D).astype(BF); return d
def setup_inputs_spread(rng):
    d = setup_inputs(rng); k = (N, 8, 1, D)
    z = (np.exp2(rng.integers(-2, 3, k)) * (rng.random(k) > 0.03125)).astype(np.float32)
    d["mat"] = (sized(rng).reshape(N, 8, 16, D) * z).reshape(N, 128, D).astype(BF); return d
def check_inputs(d):
    bad = []; h = d["hs"].reshape(N, 8, 16, 2)
    if not (np.abs(d["mat"].astype(np.float32)) <= 8192).all(): bad.append("size of mat")
    if not ((d["ids"] >= 0) & (d["ids"] <= 65535)).all(): bad.append("range of ids")
    if not ((h >= 0) & (h <= np.array([255, 65535]))).all(): bad.append("range of hs")
    if not (h == h[:, :, :1]).all(): bad.append("rows of hs alike in a group")
    return bad
def reference(mat, ids, hs):
    y = np.zeros((N, 32, K), np.float64); m = mat.astype(np.float64).reshape(N, 8, 16, D); h = hs.astype(np.int64)[:, ::16]
    for r in range(N):
        i = gentries(ids[r]).astype(np.int64)
        v = np.zeros((8, 4, K), np.float64); v[:, 0] = 1
        for q in range(N):
            t = ((i * h[q, :, :1] + h[q, :, 1:]) >> SH) & (D - 1)
            x = np.take_along_axis(m[q], t[:, None, :], 2).reshape(8, 4, 4, K)
            v = np.sum(v[:, :, None, :] * x, axis=1)
        y[r] = v.reshape(32, K)
    return {"y": y.astype(np.float32)}

@@ -1,0 +1,200 @@
+from concourse.bass import DstId, RemoteDMATransfer
+from concourse.mybir import AluOpType, ActivationFunctionType
+
+K, D = 256, 4096
+L = K // 16
+H = K // 2
+NS = 4
+W = K // NS
+GROUPS = [(1, 2), (3, 4), (5, 6, 7)]
+
+SCRATCH = {
+    "idd": ("dram", [128, L], "int32"),
+    "idl": ("sbuf", [128, 8 * L], "int32"),
+    "hsi": ("sbuf", [128, 2], "int32"),
+    "hsf": ("sbuf", [128, 2], "float32"),
+    "t1": ("sbuf", [128, 8 * L], "int32"),
+    "t2": ("sbuf", [128, 8 * L], "int32"),
+    "off": ("sbuf", [128, 8 * L], "uint16"),
+    "tab": ("sbuf", [128, D], "bfloat16"),
+    "pk": ("sbuf", [128, 8 * K], "bfloat16"),
+    "ld": ("sbuf", [128, 8 * K], "bfloat16"),
+    "s32": ("sbuf", [128, 32], "float32"),
+    "z32": ("sbuf", [128, 32], "float32"),
+    "sf": ("sbuf", [128, 128], "float32"),
+    "s0": ("sbuf", [128, 128], "bfloat16"),
+    "pr": ("sbuf", [128, K], "float32"),
+    "yt": ("sbuf", [128, 64], "float32"),
+    "ps0": ("psum", [128, 512], "float32"),
+    "ps1": ("psum", [128, 512], "float32"),
+    "ps2": ("psum", [128, 512], "float32"),
+    "ps3": ("psum", [128, 512], "float32"),
+}
+SEMAPHORES = (["ldd", "ldi", "ldh", "ldm", "sent", "h", "off_s", "sel", "ms", "expd", "o0", "o1",
+               "ya", "yb", "sta", "stb", "g7b"]
+              + ["v_s%d" % b for b in range(NS)]
+              + ["t_s%d" % b for b in range(NS)]
+              + ["id%d" % i for i in range(len(GROUPS))]
+              + ["gk%d" % k for k in range(8)]
+              + ["pk_s%d" % q for q in range(8)])
+
+
+def bits(engines):
+    m = 0
+    for e in engines:
+        m |= 1 << e
+    return m
+
+
+def dst(topo, d, core):
+    rid, pid = topo.addr(d, core)
+    return DstId(rid=rid, pnc=pid)
+
+
+def rank_program(g, core, T, topo):
+    rank = T.rank_of(core)
+    if rank is None:
+        return
+    peer = [T.cores[rank ^ k] for k in range(8)]
+    S = T.sem
+    V, P, A = g.vector, g.tensor, g.scalar
+    copy = ActivationFunctionType.Copy
+    mult, add = AluOpType.mult, AluOpType.add
+
+    g.sync.dma_start(T.idd[:], T.ids[:]).then_inc(S.ldd, 16)
+    A.dma_start(T.idl[:, 0:L], T.ids[:]).then_inc(S.ldi, 16)
+    A.dma_start(T.hsi[:], T.hs[:]).then_inc(S.ldh, 16)
+    g.sync.dma_start(T.tab[:, 0:D // 2], T.mat[:, 0:D // 2]).then_inc(S.ldm, 16)
+    g.sync.wait_ge(S.ldd, 16)
+    g.sync.dma_start(T.tab[:, D // 2:D], T.mat[:, D // 2:D]).then_inc(S.ldm, 16)
+
+    sent = 0
+    g.wait_ge(S.ldd, 16)
+    for i, ks in enumerate(GROUPS):
+        eng = topo.engines(core, peer[ks[0]])
+        g.remote_dma_fused([RemoteDMATransfer(
+            dst_ids=[dst(topo, peer[k], core) for k in ks], dma_engine_mask=bits(eng), remote_sem=S["id%d" % i],
+            srcs=[T.idd[:]], dsts=[T.idl[:, k * L:(k + 1) * L] for k in ks])], local_sem=S.sent)
+        sent += len(eng)
+    g.wait_ge(S.ms, 2)
+    g.affine_select(T.z32[:], T.z32[:], [[-16, 8], [-1, 4]], AluOpType.not_equal, 1.0, 0, 1).then_inc(S.sel, 1)
+    for a in range(4):
+        g.affine_select(T.s32[:], T.s32[:], [[-16, 8], [-1, 4]], AluOpType.not_equal, 1.0, -4 * a, 1).then_inc(S.sel, 1)
+        g.wait_ge(S.sel, a + 2)
+    for ks in [(1, 2), (3, 4), (5, 6), (7,)]:
+        for k in ks:
+            g.wait_ge(S["gk%d" % k], 1)
+            if k == 7:
+                g.wait_ge(S.g7b, 1)
+        tr = []
+        for i, k in enumerate(ks):
+            eng = topo.engines(core, peer[k])
+            n = len(eng) // len(ks)
+            eng = eng[i * n:(i + 1) * n]
+            tr.append(RemoteDMATransfer(
+                dst_ids=[dst(topo, peer[k], core)], dma_engine_mask=bits(eng), remote_sem=S["pk_s%d" % rank],
+                srcs=[T.pk[:, k * K:(k + 1) * K]], dsts=[T.ld[:, rank * K:(rank + 1) * K]]))
+            sent += n
+        g.remote_dma_fused(tr, local_sem=S.sent)
+    g.wait_ge(S.sent, sent)
+
+    h = [0]
+
+    def hashes(k0, k1, n):
+        c = slice(k0 * L, k1 * L)
+        V.tensor_scalar(T.t1[:, c], T.idl[:, c], T.hsf[:, 0:1], T.hsf[:, 1:2], mult, add).then_inc(S.h, 1)
+        h[0] += 1
+        V.wait_ge(S.h, h[0])
+        V.tensor_scalar(T.t2[:, c], T.t1[:, c], 2, D - 1, AluOpType.logical_shift_right, AluOpType.bitwise_and).then_inc(S.h, 1)
+        h[0] += 1
+        V.wait_ge(S.h, h[0])
+        V.tensor_copy(T.off[:, c], T.t2[:, c]).then_inc(S.off_s, 1)
+        V.wait_ge(S.off_s, n)
+
+    def win(o0, o1):
+        return T.tab[:, 0:D].indirect(T.off[:, o0:o1])
+
+    def gather_v(o0, o1, sem):
+        V.tensor_copy(T.pk[:, 16 * o0:16 * o1], win(o0, o1)).then_inc(sem, 1)
+
+    def gather_a(o0, o1, sem):
+        A.activation(T.pk[:, 16 * o0:16 * o1], win(o0, o1), copy).then_inc(sem, 1)
+
+    V.memset(T.z32[:], 0.0).then_inc(S.ms, 1)
+    V.memset(T.s32[:], 0.0).then_inc(S.ms, 1)
+    V.wait_ge(S.ldh, 16)
+    V.tensor_copy(T.hsf[:], T.hsi[:]).then_inc(S.h, 1)
+    h[0] += 1
+    V.wait_ge(S.h, 1)
+    V.wait_ge(S.ldi, 16)
+    hashes(0, 1, 1)
+    A.wait_ge(S.ldm, 32)
+    A.wait_ge(S.off_s, 1)
+    gather_a(0, L, S.gk0)
+    V.wait_ge(S.ldm, 32)
+    for i, ks in enumerate(GROUPS):
+        V.wait_ge(S["id%d" % i], len(topo.engines(core, peer[ks[0]])) * len(ks))
+        hashes(ks[0], ks[-1] + 1, i + 2)
+        A.wait_ge(S.off_s, i + 2)
+        gather_v(ks[0] * L, (ks[0] + 1) * L, S["gk%d" % ks[0]])
+        gather_a(ks[1] * L, (ks[1] + 1) * L, S["gk%d" % ks[1]])
+    gather_v(7 * L, 7 * L + L // 2, S.gk7)
+    gather_a(7 * L + L // 2, 8 * L, S.g7b)
+    V.wait_ge(S.sel, 5)
+    for c in range(4):
+        V.tensor_copy(T.s0[:, c:128:4], T.z32[:]).then_inc(S.expd, 1)
+    for c in range(4):
+        V.tensor_copy(T.sf[:, c:128:4], T.s32[:]).then_inc(S.expd, 1)
+
+    def arrived(q, queue):
+        k = rank ^ q
+        if k == 0:
+            queue.wait_ge(S.gk0, 1)
+        else:
+            n = len(topo.engines(T.cores[q], core))
+            queue.wait_ge(S["pk_s%d" % q], n if k == 7 else n // 2)
+
+    def pick(q, b):
+        if q == rank:
+            return T.pk[:, b * W:(b + 1) * W]
+        return T.ld[:, q * K + b * W:q * K + (b + 1) * W]
+
+    ps = [T.ps0, T.ps1, T.ps2, T.ps3]
+    vs = [S["v_s%d" % b] for b in range(NS)]
+    ts = [S["t_s%d" % b] for b in range(NS)]
+    outs = [S.o0, S.o1]
+    P.wait_ge(S.expd, 8)
+    arrived(0, P)
+    for b in range(NS):
+        P.matmul(ps[b][:, 0:W], T.s0[:], pick(0, b), True, True).then_inc(ts[b], 1)
+    for q in range(1, 8):
+        arrived(q, V)
+        for b in range(NS):
+            pr = T.pr[:, b * W:(b + 1) * W]
+            V.wait_ge(ts[b], q)
+            V.tensor_tensor(pr, ps[b][:, 0:W], pick(q, b), mult).then_inc(vs[b], 1)
+            P.wait_ge(vs[b], q)
+            if q < 7:
+                P.matmul(ps[b][:, 0:W], T.sf[:], pr, True, True).then_inc(ts[b], 1)
+            elif b % 2:
+                P.matmul(ps[b - 1][:, 0:32], T.pr[:, (b - 1) * W:(b + 1) * W], T.s32[:], True, True).then_inc(outs[b // 2], 1)
+
+    for b, sem in ((0, S.ya), (1, S.yb)):
+        V.wait_ge(outs[b], 1)
+        V.transpose(T.yt[:, 32 * b:32 * (b + 1)], ps[2 * b][:, 0:32]).then_inc(sem, 1)
+
+    def store(queue, b, blocks, sem):
+        for i in blocks:
+            j = H * b + 32 * i
+            queue.dma_start(T.y[:, j:j + 32], T.yt[32 * i:32 * (i + 1), 32 * b:32 * (b + 1)]).then_inc(sem, 16)
+
+    A.wait_ge(S.ya, 1)
+    store(A, 0, (0, 1), S.sta)
+    A.wait_ge(S.yb, 1)
+    store(A, 1, (0, 1), S.sta)
+    A.wait_ge(S.sta, 64)
+    g.sync.wait_ge(S.ya, 1)
+    store(g.sync, 0, (2, 3), S.stb)
+    g.sync.wait_ge(S.yb, 1)
+    store(g.sync, 1, (2, 3), S.stb)
+    g.sync.wait_ge(S.stb, 64)

@@ -1,12 +1,17 @@
 from concourse.bass import DstId, RemoteDMATransfer
 from concourse.mybir import AluOpType, ActivationFunctionType
 
+N = 8
 K, D = 256, 4096
 L = K // 16
 H = K // 2
 NS = 4
 W = K // NS
-GROUPS = [(1, 2), (3, 4), (5, 6, 7)]
+NH = 2
+FIRST_IDS = 2
+DIRECT_IDS = 4
+SLOTS = [(1, 2), (3, 4), (5, 6), (7,)]
+RELAY_SLOTS = [3] * N
 
 SCRATCH = {
     "idd": ("dram", [128, L], "int32"),
@@ -19,8 +24,11 @@ SCRATCH = {
     "tab": ("sbuf", [128, D], "bfloat16"),
     "pk": ("sbuf", [128, 8 * K], "bfloat16"),
     "ld": ("sbuf", [128, 8 * K], "bfloat16"),
+    "im": ("sbuf", [128, 128], "float32"),
+    "ip": ("sbuf", [128, 1], "int32"),
+    "kk": ("sbuf", [128, 3], "int32"),
+    "key": ("sbuf", [128, 2], "float32"),
     "s32": ("sbuf", [128, 32], "float32"),
-    "z32": ("sbuf", [128, 32], "float32"),
     "sf": ("sbuf", [128, 128], "float32"),
     "s0": ("sbuf", [128, 128], "bfloat16"),
     "pr": ("sbuf", [128, K], "float32"),
@@ -30,12 +38,12 @@ SCRATCH = {
     "ps2": ("psum", [128, 512], "float32"),
     "ps3": ("psum", [128, 512], "float32"),
 }
-SEMAPHORES = (["ldd", "ldi", "ldh", "ldm", "sent", "h", "off_s", "sel", "ms", "expd", "o0", "o1",
-               "ya", "yb", "sta", "stb", "g7b"]
+SEMAPHORES = (["ldd", "ldi", "ldh", "ldm", "sent", "h", "off_s", "io_s", "cs", "o0", "o1",
+               "ya", "yb", "sta", "stb", "g7b", "ida", "hid"]
               + ["v_s%d" % b for b in range(NS)]
               + ["t_s%d" % b for b in range(NS)]
-              + ["id%d" % i for i in range(len(GROUPS))]
               + ["gk%d" % k for k in range(8)]
+              + ["hp%d" % k for k in range(8)]
               + ["pk_s%d" % q for q in range(8)])
 
 
@@ -51,65 +59,148 @@ def dst(topo, d, core):
     return DstId(rid=rid, pnc=pid)
 
 
+def helpers(T, topo, rank):
+    c = T.cores[rank]
+    return [h for h in topo.cores_of(c) if topo.die(h) != topo.die(c)
+            and all(topo.may_write(h, d) for d in T.cores if d != c)][:NH]
+
+
+def id_plan(rank):
+    others = [q for q in range(N) if q != rank]
+    far = others[DIRECT_IDS:]
+    return others[:DIRECT_IDS], [far[j::NH] for j in range(NH)]
+
+
+def relayed(rank):
+    return {SLOTS[s][1]: s % NH for s in range(RELAY_SLOTS[rank])}
+
+
+def chip_engines(T, topo, rank):
+    c = T.cores[rank]
+    out = topo.engines(c, T.cores[rank ^ 1])
+    return [e for e in topo.engines(c, helpers(T, topo, rank)[0]) if e not in out]
+
+
+def pick_engines(T, topo, q, k):
+    if k in relayed(q):
+        return topo.engines(helpers(T, topo, q)[relayed(q)[k]], T.cores[q ^ k])
+    eng = topo.engines(T.cores[q], T.cores[q ^ k])
+    ks = [j for j in [s for s in SLOTS if k in s][0] if j not in relayed(q)]
+    n = len(eng) // len(ks)
+    return eng[ks.index(k) * n:(ks.index(k) + 1) * n]
+
+
+def helper_program(g, core, T, topo, rank, j):
+    S = T.sem
+    n_in = len(chip_engines(T, topo, rank))
+    sent = 0
+    far = id_plan(rank)[1][j]
+    if far:
+        g.wait_ge(S.hid, n_in)
+        eng = topo.engines(core, T.cores[far[0]])
+        g.remote_dma_fused([RemoteDMATransfer(
+            dst_ids=[dst(topo, T.cores[q], core) for q in far], dma_engine_mask=bits(eng), remote_sem=S.ida,
+            srcs=[T.idd[:]], dsts=[T.idl[:, (q ^ rank) * L:((q ^ rank) + 1) * L] for q in far])], local_sem=S.sent)
+        sent += len(eng)
+    for k, jj in sorted(relayed(rank).items()):
+        if jj == j:
+            g.wait_ge(S["hp%d" % k], n_in)
+            eng = pick_engines(T, topo, rank, k)
+            g.remote_dma_fused([RemoteDMATransfer(
+                dst_ids=[dst(topo, T.cores[rank ^ k], core)], dma_engine_mask=bits(eng), remote_sem=S["pk_s%d" % rank],
+                srcs=[T.pk[:, k * K:(k + 1) * K]], dsts=[T.ld[:, rank * K:(rank + 1) * K]])], local_sem=S.sent)
+            sent += len(eng)
+    if sent:
+        g.wait_ge(S.sent, sent)
+
+
 def rank_program(g, core, T, topo):
     rank = T.rank_of(core)
     if rank is None:
+        for r in range(N):
+            hs = helpers(T, topo, r)
+            if core in hs:
+                helper_program(g, core, T, topo, r, hs.index(core))
         return
     peer = [T.cores[rank ^ k] for k in range(8)]
+    hs = helpers(T, topo, rank)
+    inner = chip_engines(T, topo, rank)
     S = T.sem
     V, P, A = g.vector, g.tensor, g.scalar
     copy = ActivationFunctionType.Copy
     mult, add = AluOpType.mult, AluOpType.add
+    shr, band, eq = AluOpType.logical_shift_right, AluOpType.bitwise_and, AluOpType.is_equal
 
     g.sync.dma_start(T.idd[:], T.ids[:]).then_inc(S.ldd, 16)
     A.dma_start(T.idl[:, 0:L], T.ids[:]).then_inc(S.ldi, 16)
     A.dma_start(T.hsi[:], T.hs[:]).then_inc(S.ldh, 16)
     g.sync.dma_start(T.tab[:, 0:D // 2], T.mat[:, 0:D // 2]).then_inc(S.ldm, 16)
-    g.sync.wait_ge(S.ldd, 16)
     g.sync.dma_start(T.tab[:, D // 2:D], T.mat[:, D // 2:D]).then_inc(S.ldm, 16)
 
+    g.iota(T.ip[:], [[0, 1]], 0, 1).then_inc(S.io_s, 1)
+    g.iota(T.im[:], [[1, 32], [0, 4]], 0, 0, allow_small_or_imprecise_dtypes=True).then_inc(S.io_s, 1)
     sent = 0
+    near, far = id_plan(rank)
     g.wait_ge(S.ldd, 16)
-    for i, ks in enumerate(GROUPS):
-        eng = topo.engines(core, peer[ks[0]])
+    eng = topo.engines(core, T.cores[near[0]])
+
+    def ids_to(qs):
         g.remote_dma_fused([RemoteDMATransfer(
-            dst_ids=[dst(topo, peer[k], core) for k in ks], dma_engine_mask=bits(eng), remote_sem=S["id%d" % i],
-            srcs=[T.idd[:]], dsts=[T.idl[:, k * L:(k + 1) * L] for k in ks])], local_sem=S.sent)
-        sent += len(eng)
-    g.wait_ge(S.ms, 2)
-    g.affine_select(T.z32[:], T.z32[:], [[-16, 8], [-1, 4]], AluOpType.not_equal, 1.0, 0, 1).then_inc(S.sel, 1)
-    for a in range(4):
-        g.affine_select(T.s32[:], T.s32[:], [[-16, 8], [-1, 4]], AluOpType.not_equal, 1.0, -4 * a, 1).then_inc(S.sel, 1)
-        g.wait_ge(S.sel, a + 2)
-    for ks in [(1, 2), (3, 4), (5, 6), (7,)]:
+            dst_ids=[dst(topo, T.cores[q], core) for q in qs], dma_engine_mask=bits(eng), remote_sem=S.ida,
+            srcs=[T.idd[:]], dsts=[T.idl[:, (q ^ rank) * L:((q ^ rank) + 1) * L] for q in qs])], local_sem=S.sent)
+        return len(eng)
+
+    sent += ids_to(near[:FIRST_IDS])
+    to = [h for h, f in zip(hs, far) if f]
+    if to:
+        g.remote_dma_fused([RemoteDMATransfer(
+            dst_ids=[dst(topo, h, core) for h in to], dma_engine_mask=bits(inner), remote_sem=S.hid,
+            srcs=[T.idd[:]], dsts=[T.idd[:] for h in to])], local_sem=S.sent)
+        sent += len(inner)
+    if near[FIRST_IDS:]:
+        sent += ids_to(near[FIRST_IDS:])
+    for ks in SLOTS:
+        tr = []
         for k in ks:
             g.wait_ge(S["gk%d" % k], 1)
             if k == 7:
                 g.wait_ge(S.g7b, 1)
-        tr = []
-        for i, k in enumerate(ks):
-            eng = topo.engines(core, peer[k])
-            n = len(eng) // len(ks)
-            eng = eng[i * n:(i + 1) * n]
-            tr.append(RemoteDMATransfer(
-                dst_ids=[dst(topo, peer[k], core)], dma_engine_mask=bits(eng), remote_sem=S["pk_s%d" % rank],
-                srcs=[T.pk[:, k * K:(k + 1) * K]], dsts=[T.ld[:, rank * K:(rank + 1) * K]]))
-            sent += n
+            src = T.pk[:, k * K:(k + 1) * K]
+            if k in relayed(rank):
+                tr.append(RemoteDMATransfer(
+                    dst_ids=[dst(topo, hs[relayed(rank)[k]], core)], dma_engine_mask=bits(inner),
+                    remote_sem=S["hp%d" % k], srcs=[src], dsts=[src]))
+                sent += len(inner)
+            else:
+                eng = pick_engines(T, topo, rank, k)
+                tr.append(RemoteDMATransfer(
+                    dst_ids=[dst(topo, peer[k], core)], dma_engine_mask=bits(eng), remote_sem=S["pk_s%d" % rank],
+                    srcs=[src], dsts=[T.ld[:, rank * K:(rank + 1) * K]]))
+                sent += len(eng)
         g.remote_dma_fused(tr, local_sem=S.sent)
     g.wait_ge(S.sent, sent)
 
     h = [0]
 
-    def hashes(k0, k1, n):
-        c = slice(k0 * L, k1 * L)
-        V.tensor_scalar(T.t1[:, c], T.idl[:, c], T.hsf[:, 0:1], T.hsf[:, 1:2], mult, add).then_inc(S.h, 1)
+    def step(ins, n=1):
+        ins.then_inc(S.h, 1)
         h[0] += 1
+
+    def settle():
         V.wait_ge(S.h, h[0])
-        V.tensor_scalar(T.t2[:, c], T.t1[:, c], 2, D - 1, AluOpType.logical_shift_right, AluOpType.bitwise_and).then_inc(S.h, 1)
-        h[0] += 1
-        V.wait_ge(S.h, h[0])
-        V.tensor_copy(T.off[:, c], T.t2[:, c]).then_inc(S.off_s, 1)
-        V.wait_ge(S.off_s, n)
+
+    V.wait_ge(S.io_s, 2)
+    step(V.tensor_scalar(T.kk[:, 0:1], T.ip[:], 2, 28, shr, band))
+    step(V.tensor_scalar(T.kk[:, 1:2], T.ip[:], 3, None, band))
+    step(V.tensor_scalar(T.kk[:, 2:3], T.ip[:], 12, None, band))
+    settle()
+    step(V.tensor_tensor(T.key[:, 0:1], T.kk[:, 0:1], T.kk[:, 1:2], add))
+    settle()
+    step(V.tensor_scalar(T.key[:, 1:2], T.kk[:, 2:3], 64.0, T.key[:, 0:1], mult, add))
+    V.tensor_scalar(T.sf[:], T.im[:], T.key[:, 0:1], None, eq).then_inc(S.cs, 1)
+    V.tensor_scalar(T.s32[:], T.im[:, 0:128:4], T.key[:, 0:1], None, eq).then_inc(S.cs, 1)
+    settle()
+    V.tensor_scalar(T.s0[:], T.im[:], T.key[:, 1:2], None, eq).then_inc(S.cs, 1)
 
     def win(o0, o1):
         return T.tab[:, 0:D].indirect(T.off[:, o0:o1])
@@ -120,39 +211,32 @@ def rank_program(g, core, T, topo):
     def gather_a(o0, o1, sem):
         A.activation(T.pk[:, 16 * o0:16 * o1], win(o0, o1), copy).then_inc(sem, 1)
 
-    V.memset(T.z32[:], 0.0).then_inc(S.ms, 1)
-    V.memset(T.s32[:], 0.0).then_inc(S.ms, 1)
     V.wait_ge(S.ldh, 16)
-    V.tensor_copy(T.hsf[:], T.hsi[:]).then_inc(S.h, 1)
-    h[0] += 1
-    V.wait_ge(S.h, 1)
+    step(V.tensor_copy(T.hsf[:], T.hsi[:]))
+    settle()
     V.wait_ge(S.ldi, 16)
-    hashes(0, 1, 1)
-    A.wait_ge(S.ldm, 32)
-    A.wait_ge(S.off_s, 1)
-    gather_a(0, L, S.gk0)
-    V.wait_ge(S.ldm, 32)
-    for i, ks in enumerate(GROUPS):
-        V.wait_ge(S["id%d" % i], len(topo.engines(core, peer[ks[0]])) * len(ks))
-        hashes(ks[0], ks[-1] + 1, i + 2)
-        A.wait_ge(S.off_s, i + 2)
+    V.wait_ge(S.ida, sum(len(topo.engines(c, core)) for c in peer[1:]))
+    step(V.tensor_scalar(T.t1[:], T.idl[:], T.hsf[:, 0:1], T.hsf[:, 1:2], mult, add))
+    settle()
+    step(V.tensor_scalar(T.t2[:], T.t1[:], 2, D - 1, shr, band))
+    settle()
+    V.tensor_copy(T.off[:], T.t2[:]).then_inc(S.off_s, 1)
+    for E in (V, A):
+        E.wait_ge(S.off_s, 1)
+        E.wait_ge(S.ldm, 32)
+    for ks in SLOTS[:-1]:
         gather_v(ks[0] * L, (ks[0] + 1) * L, S["gk%d" % ks[0]])
         gather_a(ks[1] * L, (ks[1] + 1) * L, S["gk%d" % ks[1]])
     gather_v(7 * L, 7 * L + L // 2, S.gk7)
     gather_a(7 * L + L // 2, 8 * L, S.g7b)
-    V.wait_ge(S.sel, 5)
-    for c in range(4):
-        V.tensor_copy(T.s0[:, c:128:4], T.z32[:]).then_inc(S.expd, 1)
-    for c in range(4):
-        V.tensor_copy(T.sf[:, c:128:4], T.s32[:]).then_inc(S.expd, 1)
+    gather_a(0, L, S.gk0)
 
     def arrived(q, queue):
         k = rank ^ q
         if k == 0:
             queue.wait_ge(S.gk0, 1)
         else:
-            n = len(topo.engines(T.cores[q], core))
-            queue.wait_ge(S["pk_s%d" % q], n if k == 7 else n // 2)
+            queue.wait_ge(S["pk_s%d" % q], len(pick_engines(T, topo, q, k)))
 
     def pick(q, b):
         if q == rank:
@@ -163,7 +247,7 @@ def rank_program(g, core, T, topo):
     vs = [S["v_s%d" % b] for b in range(NS)]
     ts = [S["t_s%d" % b] for b in range(NS)]
     outs = [S.o0, S.o1]
-    P.wait_ge(S.expd, 8)
+    P.wait_ge(S.cs, 3)
     arrived(0, P)
     for b in range(NS):
         P.matmul(ps[b][:, 0:W], T.s0[:], pick(0, b), True, True).then_inc(ts[b], 1)

@@ -7,11 +7,11 @@ L = K // 16
 H = K // 2
 NS = 4
 W = K // NS
-NH = 2
 FIRST_IDS = 2
 DIRECT_IDS = 4
-SLOTS = [(1, 2), (3, 4), (5, 6), (7,)]
-RELAY_SLOTS = [3] * N
+LOW = [[(6, "far")], [(3, "far"), (2, "near")], [(4, "far")], [(7, "out"), (5, "out")], [(1, "out")]]
+HIGH = [[(6, "far"), (2, "near")], [(3, "far"), (7, "out")], [(4, "far"), (5, "out")], [(1, "out")]]
+HALVED = 2
 
 SCRATCH = {
     "idd": ("dram", [128, L], "int32"),
@@ -26,25 +26,23 @@ SCRATCH = {
     "ld": ("sbuf", [128, 8 * K], "bfloat16"),
     "im": ("sbuf", [128, 128], "float32"),
     "ip": ("sbuf", [128, 1], "int32"),
-    "kk": ("sbuf", [128, 3], "int32"),
-    "key": ("sbuf", [128, 2], "float32"),
+    "kk": ("sbuf", [128, 2], "int32"),
+    "key": ("sbuf", [128, 1], "float32"),
     "s32": ("sbuf", [128, 32], "float32"),
     "sf": ("sbuf", [128, 128], "float32"),
-    "s0": ("sbuf", [128, 128], "bfloat16"),
     "pr": ("sbuf", [128, K], "float32"),
-    "yt": ("sbuf", [128, 64], "float32"),
+    "yt": ("sbuf", [128, 32], "float32"),
+    "yu": ("sbuf", [128, H], "float32"),
     "ps0": ("psum", [128, 512], "float32"),
     "ps1": ("psum", [128, 512], "float32"),
     "ps2": ("psum", [128, 512], "float32"),
     "ps3": ("psum", [128, 512], "float32"),
 }
-SEMAPHORES = (["ldd", "ldi", "ldh", "ldm", "sent", "h", "off_s", "io_s", "cs", "o0", "o1",
-               "ya", "yb", "sta", "stb", "g7b", "ida", "hid"]
+SEMAPHORES = (["ldd", "ldi", "ldh", "ldm", "sent", "h", "h0", "h1", "io_s", "cs", "o0", "o1", "o2",
+               "ya", "yb", "yc", "sta", "stb", "ida", "hid"]
               + ["v_s%d" % b for b in range(NS)]
               + ["t_s%d" % b for b in range(NS)]
-              + ["gk%d" % k for k in range(8)]
-              + ["hp%d" % k for k in range(8)]
-              + ["pk_s%d" % q for q in range(8)])
+              + [name % k + x for name in ("gk%d", "hp%d", "pk_s%d") for k in range(N) for x in "ab"])
 
 
 def bits(engines):
@@ -59,57 +57,94 @@ def dst(topo, d, core):
     return DstId(rid=rid, pnc=pid)
 
 
-def helpers(T, topo, rank):
+def slots(q):
+    return LOW
+
+
+def pos(q, k):
+    return ([j for s in slots(q) for j, way in s] + [0]).index(k)
+
+
+def id_block(T, q, k):
+    return T.idl[:, pos(q, k) * L:(pos(q, k) + 1) * L]
+
+
+def pieces(q, k):
+    return [(0, H, "a"), (H, K, "b")] if k in [j for s in slots(q)[1:] for j, way in s if way != "out"] else [(0, K, "a")]
+
+
+def engine_sets(T, topo, rank):
     c = T.cores[rank]
-    return [h for h in topo.cores_of(c) if topo.die(h) != topo.die(c)
-            and all(topo.may_write(h, d) for d in T.cores if d != c)][:NH]
-
-
-def id_plan(rank):
-    others = [q for q in range(N) if q != rank]
-    far = others[DIRECT_IDS:]
-    return others[:DIRECT_IDS], [far[j::NH] for j in range(NH)]
-
-
-def relayed(rank):
-    return {SLOTS[s][1]: s % NH for s in range(RELAY_SLOTS[rank])}
-
-
-def chip_engines(T, topo, rank):
-    c = T.cores[rank]
+    every = topo.engines(c, [h for h in topo.cores_of(c) if h != c][0])
     out = topo.engines(c, T.cores[rank ^ 1])
-    return [e for e in topo.engines(c, helpers(T, topo, rank)[0]) if e not in out]
+    return every, out, [e for e in every if e not in out]
 
 
-def pick_engines(T, topo, q, k):
-    if k in relayed(q):
-        return topo.engines(helpers(T, topo, q)[relayed(q)[k]], T.cores[q ^ k])
-    eng = topo.engines(T.cores[q], T.cores[q ^ k])
-    ks = [j for j in [s for s in SLOTS if k in s][0] if j not in relayed(q)]
-    n = len(eng) // len(ks)
-    return eng[ks.index(k) * n:(ks.index(k) + 1) * n]
+def plan(T, topo, rank):
+    c = T.cores[rank]
+    every, out, inner = engine_sets(T, topo, rank)
+
+    def reach(h):
+        return sum(topo.may_write(h, d) for d in T.cores if d != c)
+
+    free = sorted((h for h in topo.cores_of(c) if h != c), key=reach)
+    todo = sorted(((k, way) for s in slots(rank) for k, way in s if way != "out"),
+                  key=lambda e: (topo.same_plane(c, T.cores[rank ^ e[0]]), e[1] == "far"))
+    helper = {}
+    others = [q for q in range(DIRECT_IDS, N) if q != rank]
+    strict = [q for q in others if not topo.same_plane(c, T.cores[q])]
+    for k, way in todo:
+        if len(helper) == len(others):
+            helper[k] = helper[slots(rank)[0][0][0]]
+            continue
+        fit = [h for h in free if (topo.die(h) == topo.die(c)) == (way == "near") and topo.may_write(h, T.cores[rank ^ k])]
+        short = len(strict) > sum(reach(h) == N - 1 for h in helper.values())
+        helper[k] = fit[-1] if short and way == "far" else fit[0]
+        free.remove(helper[k])
+    far, hs = {}, sorted(set(helper.values()), key=reach)
+    for q in others:
+        h = [h for h in hs if topo.may_write(h, T.cores[q])][0]
+        hs.remove(h)
+        far[h] = q
+    ways = {}
+    for s in slots(rank):
+        for i, (k, way) in enumerate(s):
+            if len(s) == 1:
+                eng = out if way == "out" else every
+            elif s[0][1] == "out":
+                eng = out[i * len(out) // 2:(i + 1) * len(out) // 2]
+            else:
+                eng = out if i else inner
+            h = helper.get(k)
+            ways[k] = (h, eng, eng if h is None else topo.engines(h, T.cores[rank ^ k]))
+    return [q for q in range(DIRECT_IDS) if q != rank], far, ways
 
 
-def helper_program(g, core, T, topo, rank, j):
+def write(topo, core, cores, engines, sem, src, dsts):
+    return RemoteDMATransfer(dst_ids=[dst(topo, c, core) for c in cores], dma_engine_mask=bits(engines),
+                             remote_sem=sem, srcs=[src], dsts=dsts)
+
+
+def helper_program(g, core, T, topo, rank):
     S = T.sem
-    n_in = len(chip_engines(T, topo, rank))
+    near, far, ways = plan(T, topo, rank)
     sent = 0
-    far = id_plan(rank)[1][j]
-    if far:
-        g.wait_ge(S.hid, n_in)
-        eng = topo.engines(core, T.cores[far[0]])
-        g.remote_dma_fused([RemoteDMATransfer(
-            dst_ids=[dst(topo, T.cores[q], core) for q in far], dma_engine_mask=bits(eng), remote_sem=S.ida,
-            srcs=[T.idd[:]], dsts=[T.idl[:, (q ^ rank) * L:((q ^ rank) + 1) * L] for q in far])], local_sem=S.sent)
+    if core in far:
+        q = far[core]
+        g.wait_ge(S.hid, len(engine_sets(T, topo, rank)[2]))
+        eng = topo.engines(core, T.cores[q])
+        g.remote_dma_fused([write(topo, core, [T.cores[q]], eng, S.ida, T.idd[:], [id_block(T, q, q ^ rank)])],
+                           local_sem=S.sent)
         sent += len(eng)
-    for k, jj in sorted(relayed(rank).items()):
-        if jj == j:
-            g.wait_ge(S["hp%d" % k], n_in)
-            eng = pick_engines(T, topo, rank, k)
-            g.remote_dma_fused([RemoteDMATransfer(
-                dst_ids=[dst(topo, T.cores[rank ^ k], core)], dma_engine_mask=bits(eng), remote_sem=S["pk_s%d" % rank],
-                srcs=[T.pk[:, k * K:(k + 1) * K]], dsts=[T.ld[:, rank * K:(rank + 1) * K]])], local_sem=S.sent)
-            sent += len(eng)
+    for k, (h, feed, eng) in ways.items():
+        if h == core:
+            o = pos(rank, k) * K
+            for c0, c1, x in pieces(rank, k):
+                g.wait_ge(S["hp%d" % k + x], len(feed))
+                g.remote_dma_fused([write(topo, core, [T.cores[rank ^ k]], eng, S["pk_s%d" % rank + x],
+                                          T.pk[:, o + c0:o + c1], [T.ld[:, rank * K + c0:rank * K + c1]])],
+                                   local_sem=S.sent)
+                sent += len(eng)
     if sent:
         g.wait_ge(S.sent, sent)
 
@@ -118,13 +153,11 @@ def rank_program(g, core, T, topo):
     rank = T.rank_of(core)
     if rank is None:
         for r in range(N):
-            hs = helpers(T, topo, r)
-            if core in hs:
-                helper_program(g, core, T, topo, r, hs.index(core))
+            if core in topo.cores_of(T.cores[r]):
+                helper_program(g, core, T, topo, r)
         return
-    peer = [T.cores[rank ^ k] for k in range(8)]
-    hs = helpers(T, topo, rank)
-    inner = chip_engines(T, topo, rank)
+    near, far, ways = plan(T, topo, rank)
+    every, out, inner = engine_sets(T, topo, rank)
     S = T.sem
     V, P, A = g.vector, g.tensor, g.scalar
     copy = ActivationFunctionType.Copy
@@ -132,57 +165,46 @@ def rank_program(g, core, T, topo):
     shr, band, eq = AluOpType.logical_shift_right, AluOpType.bitwise_and, AluOpType.is_equal
 
     g.sync.dma_start(T.idd[:], T.ids[:]).then_inc(S.ldd, 16)
-    A.dma_start(T.idl[:, 0:L], T.ids[:]).then_inc(S.ldi, 16)
+    if rank == 0:
+        for i in range(16):
+            (g.sync, A)[i % 2].dma_start(T.tab[i:128:16, :], T.mat[i // 4:128:16, :]).then_inc(S.ldm, 16)
+    else:
+        g.sync.dma_start(T.tab[:], T.mat[:]).then_inc(S.ldm, 16)
     A.dma_start(T.hsi[:], T.hs[:]).then_inc(S.ldh, 16)
-    g.sync.dma_start(T.tab[:, 0:D // 2], T.mat[:, 0:D // 2]).then_inc(S.ldm, 16)
-    g.sync.dma_start(T.tab[:, D // 2:D], T.mat[:, D // 2:D]).then_inc(S.ldm, 16)
+    A.dma_start(id_block(T, rank, 0), T.ids[:]).then_inc(S.ldi, 16)
+
+    def ids_to(qs):
+        return write(topo, core, [T.cores[q] for q in qs], out, S.ida, T.idd[:], [id_block(T, q, q ^ rank) for q in qs])
 
     g.iota(T.ip[:], [[0, 1]], 0, 1).then_inc(S.io_s, 1)
     g.iota(T.im[:], [[1, 32], [0, 4]], 0, 0, allow_small_or_imprecise_dtypes=True).then_inc(S.io_s, 1)
-    sent = 0
-    near, far = id_plan(rank)
     g.wait_ge(S.ldd, 16)
-    eng = topo.engines(core, T.cores[near[0]])
-
-    def ids_to(qs):
-        g.remote_dma_fused([RemoteDMATransfer(
-            dst_ids=[dst(topo, T.cores[q], core) for q in qs], dma_engine_mask=bits(eng), remote_sem=S.ida,
-            srcs=[T.idd[:]], dsts=[T.idl[:, (q ^ rank) * L:((q ^ rank) + 1) * L] for q in qs])], local_sem=S.sent)
-        return len(eng)
-
-    sent += ids_to(near[:FIRST_IDS])
-    to = [h for h, f in zip(hs, far) if f]
-    if to:
-        g.remote_dma_fused([RemoteDMATransfer(
-            dst_ids=[dst(topo, h, core) for h in to], dma_engine_mask=bits(inner), remote_sem=S.hid,
-            srcs=[T.idd[:]], dsts=[T.idd[:] for h in to])], local_sem=S.sent)
-        sent += len(inner)
-    if near[FIRST_IDS:]:
-        sent += ids_to(near[FIRST_IDS:])
-    for ks in SLOTS:
-        tr = []
-        for k in ks:
-            g.wait_ge(S["gk%d" % k], 1)
-            if k == 7:
-                g.wait_ge(S.g7b, 1)
-            src = T.pk[:, k * K:(k + 1) * K]
-            if k in relayed(rank):
-                tr.append(RemoteDMATransfer(
-                    dst_ids=[dst(topo, hs[relayed(rank)[k]], core)], dma_engine_mask=bits(inner),
-                    remote_sem=S["hp%d" % k], srcs=[src], dsts=[src]))
-                sent += len(inner)
-            else:
-                eng = pick_engines(T, topo, rank, k)
-                tr.append(RemoteDMATransfer(
-                    dst_ids=[dst(topo, peer[k], core)], dma_engine_mask=bits(eng), remote_sem=S["pk_s%d" % rank],
-                    srcs=[src], dsts=[T.ld[:, rank * K:(rank + 1) * K]]))
+    g.remote_dma_fused([ids_to(near[:FIRST_IDS])], local_sem=S.sent)
+    g.remote_dma_fused([write(topo, core, list(far), inner, S.hid, T.idd[:], [T.idd[:] for h in far]),
+                        ids_to(near[FIRST_IDS:])], local_sem=S.sent)
+    sent = 2 * len(out) + len(inner)
+    for i, s in enumerate(slots(rank)):
+        parts = sorted(((k, piece) for k, way in s for piece in pieces(rank, k)), key=lambda p: p[1][2])
+        together = len(s) == 1
+        n = 1 if len(parts) % len(s) else len(s)
+        for call in [parts[j:j + n] for j in range(0, len(parts), n)]:
+            tr = []
+            for k, (c0, c1, x) in call:
+                h, eng, last = ways[k]
+                g.wait_ge(S["gk%d" % k + x], 2 if together else 1)
+                src = T.pk[:, pos(rank, k) * K + c0:pos(rank, k) * K + c1]
+                if h is None:
+                    tr.append(write(topo, core, [T.cores[rank ^ k]], eng, S["pk_s%d" % rank + x], src,
+                                    [T.ld[:, rank * K + c0:rank * K + c1]]))
+                else:
+                    tr.append(write(topo, core, [h], eng, S["hp%d" % k + x], src, [src]))
                 sent += len(eng)
-        g.remote_dma_fused(tr, local_sem=S.sent)
+            g.remote_dma_fused(tr, local_sem=S.sent)
     g.wait_ge(S.sent, sent)
 
     h = [0]
 
-    def step(ins, n=1):
+    def step(ins):
         ins.then_inc(S.h, 1)
         h[0] += 1
 
@@ -192,93 +214,94 @@ def rank_program(g, core, T, topo):
     V.wait_ge(S.io_s, 2)
     step(V.tensor_scalar(T.kk[:, 0:1], T.ip[:], 2, 28, shr, band))
     step(V.tensor_scalar(T.kk[:, 1:2], T.ip[:], 3, None, band))
-    step(V.tensor_scalar(T.kk[:, 2:3], T.ip[:], 12, None, band))
     settle()
-    step(V.tensor_tensor(T.key[:, 0:1], T.kk[:, 0:1], T.kk[:, 1:2], add))
+    step(V.tensor_tensor(T.key[:], T.kk[:, 0:1], T.kk[:, 1:2], add))
     settle()
-    step(V.tensor_scalar(T.key[:, 1:2], T.kk[:, 2:3], 64.0, T.key[:, 0:1], mult, add))
-    V.tensor_scalar(T.sf[:], T.im[:], T.key[:, 0:1], None, eq).then_inc(S.cs, 1)
-    V.tensor_scalar(T.s32[:], T.im[:, 0:128:4], T.key[:, 0:1], None, eq).then_inc(S.cs, 1)
-    settle()
-    V.tensor_scalar(T.s0[:], T.im[:], T.key[:, 1:2], None, eq).then_inc(S.cs, 1)
-
-    def win(o0, o1):
-        return T.tab[:, 0:D].indirect(T.off[:, o0:o1])
-
-    def gather_v(o0, o1, sem):
-        V.tensor_copy(T.pk[:, 16 * o0:16 * o1], win(o0, o1)).then_inc(sem, 1)
-
-    def gather_a(o0, o1, sem):
-        A.activation(T.pk[:, 16 * o0:16 * o1], win(o0, o1), copy).then_inc(sem, 1)
+    V.tensor_scalar(T.sf[:], T.im[:], T.key[:], None, eq).then_inc(S.cs, 1)
+    V.tensor_scalar(T.s32[:], T.im[:, 0:128:4], T.key[:], None, eq).then_inc(S.cs, 1)
 
     V.wait_ge(S.ldh, 16)
     step(V.tensor_copy(T.hsf[:], T.hsi[:]))
     settle()
     V.wait_ge(S.ldi, 16)
-    V.wait_ge(S.ida, sum(len(topo.engines(c, core)) for c in peer[1:]))
-    step(V.tensor_scalar(T.t1[:], T.idl[:], T.hsf[:, 0:1], T.hsf[:, 1:2], mult, add))
-    settle()
-    step(V.tensor_scalar(T.t2[:], T.t1[:], 2, D - 1, shr, band))
-    settle()
-    V.tensor_copy(T.off[:], T.t2[:]).then_inc(S.off_s, 1)
-    for E in (V, A):
-        E.wait_ge(S.off_s, 1)
-        E.wait_ge(S.ldm, 32)
-    for ks in SLOTS[:-1]:
-        gather_v(ks[0] * L, (ks[0] + 1) * L, S["gk%d" % ks[0]])
-        gather_a(ks[1] * L, (ks[1] + 1) * L, S["gk%d" % ks[1]])
-    gather_v(7 * L, 7 * L + L // 2, S.gk7)
-    gather_a(7 * L + L // 2, 8 * L, S.g7b)
-    gather_a(0, L, S.gk0)
+    V.wait_ge(S.ida, len(out) * (N - 1))
+    halves = [(slice(0, 4 * L), S.h0), (slice(4 * L, 8 * L), S.h1)]
+    for c, sem in halves:
+        V.tensor_scalar(T.t1[:, c], T.idl[:, c], T.hsf[:, 0:1], T.hsf[:, 1:2], mult, add).then_inc(sem, 1)
+    for c, sem in halves:
+        V.wait_ge(sem, 1)
+        V.tensor_scalar(T.t2[:, c], T.t1[:, c], 2, D - 1, shr, band).then_inc(sem, 1)
+    for c, sem in halves:
+        V.wait_ge(sem, 2)
+        V.tensor_copy(T.off[:, c], T.t2[:, c]).then_inc(sem, 1)
+    seen = {0: set(), 1: set()}
 
-    def arrived(q, queue):
-        k = rank ^ q
-        if k == 0:
-            queue.wait_ge(S.gk0, 1)
+    def gather(e, k, c0, c1, x):
+        E = (V, A)[e]
+        half = pos(rank, k) // 4
+        if half not in seen[e]:
+            E.wait_ge(halves[half][1], 3)
+            if not seen[e]:
+                E.wait_ge(S.ldm, 256 if rank == 0 else 16)
+            seen[e].add(half)
+        o0, o1 = pos(rank, k) * K + c0, pos(rank, k) * K + c1
+        win = T.tab[:, 0:D].indirect(T.off[:, o0 // 16:o1 // 16])
+        ins = V.tensor_copy(T.pk[:, o0:o1], win) if e == 0 else A.activation(T.pk[:, o0:o1], win, copy)
+        ins.then_inc(S["gk%d" % k + x], 1)
+
+    for i, s in enumerate(slots(rank)):
+        if len(s) == 1:
+            for c0, c1, x in pieces(rank, s[0][0]):
+                gather(0, s[0][0], c0, (c0 + c1) // 2, x)
+                gather(1, s[0][0], (c0 + c1) // 2, c1, x)
         else:
-            queue.wait_ge(S["pk_s%d" % q], len(pick_engines(T, topo, q, k)))
+            for e in (0, 1):
+                for piece in pieces(rank, s[e][0]):
+                    gather(e, s[e][0], *piece)
+    gather(1, 0, 0, K, "a")
+
+    def arrived(q, b):
+        for c0, c1, x in pieces(q, rank ^ q):
+            if c0 == b * W and q == rank:
+                V.wait_ge(S.gk0a, 1)
+            elif c0 == b * W:
+                V.wait_ge(S["pk_s%d" % q + x], len(plan(T, topo, q)[2][rank ^ q][2]))
 
     def pick(q, b):
-        if q == rank:
-            return T.pk[:, b * W:(b + 1) * W]
-        return T.ld[:, q * K + b * W:q * K + (b + 1) * W]
+        o = pos(rank, 0) * K if q == rank else q * K
+        return (T.pk if q == rank else T.ld)[:, o + b * W:o + (b + 1) * W]
 
     ps = [T.ps0, T.ps1, T.ps2, T.ps3]
     vs = [S["v_s%d" % b] for b in range(NS)]
     ts = [S["t_s%d" % b] for b in range(NS)]
-    outs = [S.o0, S.o1]
-    P.wait_ge(S.cs, 3)
-    arrived(0, P)
-    for b in range(NS):
-        P.matmul(ps[b][:, 0:W], T.s0[:], pick(0, b), True, True).then_inc(ts[b], 1)
-    for q in range(1, 8):
-        arrived(q, V)
+    outs = [S.o0, S.o1, S.o2]
+    P.wait_ge(S.cs, 2)
+    for q in range(1, N):
         for b in range(NS):
+            arrived(q, b)
             pr = T.pr[:, b * W:(b + 1) * W]
-            V.wait_ge(ts[b], q)
-            V.tensor_tensor(pr, ps[b][:, 0:W], pick(q, b), mult).then_inc(vs[b], 1)
+            if q == 1:
+                arrived(0, b)
+            else:
+                V.wait_ge(ts[b], q - 1)
+            V.tensor_tensor(pr, pick(0, b) if q == 1 else ps[b][:, 0:W], pick(q, b), mult).then_inc(vs[b], 1)
             P.wait_ge(vs[b], q)
-            if q < 7:
+            if q < N - 1:
                 P.matmul(ps[b][:, 0:W], T.sf[:], pr, True, True).then_inc(ts[b], 1)
-            elif b % 2:
-                P.matmul(ps[b - 1][:, 0:32], T.pr[:, (b - 1) * W:(b + 1) * W], T.s32[:], True, True).then_inc(outs[b // 2], 1)
+            elif b == 1:
+                P.matmul(ps[0][:, 0:32], T.pr[:, 0:H], T.s32[:], True, True).then_inc(outs[0], 1)
+            elif b > 1:
+                P.matmul(ps[b][0:32, 0:W], T.s32[:], pr, True, True).then_inc(outs[b - 1], 1)
 
-    for b, sem in ((0, S.ya), (1, S.yb)):
-        V.wait_ge(outs[b], 1)
-        V.transpose(T.yt[:, 32 * b:32 * (b + 1)], ps[2 * b][:, 0:32]).then_inc(sem, 1)
-
-    def store(queue, b, blocks, sem):
+    V.wait_ge(outs[0], 1)
+    V.transpose(T.yt[:], ps[0][:, 0:32]).then_inc(S.ya, 1)
+    for b, sem in ((2, S.yb), (3, S.yc)):
+        V.wait_ge(outs[b - 1], 1)
+        V.tensor_copy(T.yu[0:32, (b - 2) * W:(b - 1) * W], ps[b][0:32, 0:W]).then_inc(sem, 1)
+    for Q, blocks, b, ready, done in ((g.sync, (0, 1), 2, S.yb, S.sta), (A, (2, 3), 3, S.yc, S.stb)):
+        Q.wait_ge(S.ya, 1)
         for i in blocks:
-            j = H * b + 32 * i
-            queue.dma_start(T.y[:, j:j + 32], T.yt[32 * i:32 * (i + 1), 32 * b:32 * (b + 1)]).then_inc(sem, 16)
-
-    A.wait_ge(S.ya, 1)
-    store(A, 0, (0, 1), S.sta)
-    A.wait_ge(S.yb, 1)
-    store(A, 1, (0, 1), S.sta)
-    A.wait_ge(S.sta, 64)
-    g.sync.wait_ge(S.ya, 1)
-    store(g.sync, 0, (2, 3), S.stb)
-    g.sync.wait_ge(S.yb, 1)
-    store(g.sync, 1, (2, 3), S.stb)
-    g.sync.wait_ge(S.stb, 64)
+            Q.dma_start(T.y[:, 32 * i:32 * (i + 1)], T.yt[32 * i:32 * (i + 1), :]).then_inc(done, 16)
+        Q.wait_ge(ready, 1)
+        Q.dma_start(T.y[:, b * W:(b + 1) * W], T.yu[0:32, (b - 2) * W:(b - 1) * W]).then_inc(done, 16)
+        Q.wait_ge(done, 48)

from concourse.bass import DstId, RemoteDMATransfer
from concourse.mybir import AluOpType, ActivationFunctionType

N = 8
K, D = 256, 4096
L = K // 16
H = K // 2
NS = 4
W = K // NS
FIRST_IDS = 2
DIRECT_IDS = 4
LOW = [[(6, "far")], [(3, "far"), (2, "near")], [(4, "far")], [(7, "out"), (5, "out")], [(1, "out")]]
HIGH = [[(6, "far"), (2, "near")], [(3, "far"), (7, "out")], [(4, "far"), (5, "out")], [(1, "out")]]
HALVED = 2

SCRATCH = {
    "idd": ("dram", [128, L], "int32"),
    "idl": ("sbuf", [128, 8 * L], "int32"),
    "hsi": ("sbuf", [128, 2], "int32"),
    "hsf": ("sbuf", [128, 2], "float32"),
    "t1": ("sbuf", [128, 8 * L], "int32"),
    "t2": ("sbuf", [128, 8 * L], "int32"),
    "off": ("sbuf", [128, 8 * L], "uint16"),
    "tab": ("sbuf", [128, D], "bfloat16"),
    "pk": ("sbuf", [128, 8 * K], "bfloat16"),
    "ld": ("sbuf", [128, 8 * K], "bfloat16"),
    "im": ("sbuf", [128, 128], "float32"),
    "ip": ("sbuf", [128, 1], "int32"),
    "kk": ("sbuf", [128, 2], "int32"),
    "key": ("sbuf", [128, 1], "float32"),
    "s32": ("sbuf", [128, 32], "float32"),
    "sf": ("sbuf", [128, 128], "float32"),
    "pr": ("sbuf", [128, K], "float32"),
    "yt": ("sbuf", [128, 32], "float32"),
    "yu": ("sbuf", [128, H], "float32"),
    "ps0": ("psum", [128, 512], "float32"),
    "ps1": ("psum", [128, 512], "float32"),
    "ps2": ("psum", [128, 512], "float32"),
    "ps3": ("psum", [128, 512], "float32"),
}
SEMAPHORES = (["ldd", "ldi", "ldh", "ldm", "sent", "h", "h0", "h1", "io_s", "cs", "o0", "o1", "o2",
               "ya", "yb", "yc", "sta", "stb", "ida", "hid"]
              + ["v_s%d" % b for b in range(NS)]
              + ["t_s%d" % b for b in range(NS)]
              + [name % k + x for name in ("gk%d", "hp%d", "pk_s%d") for k in range(N) for x in "ab"])


def bits(engines):
    m = 0
    for e in engines:
        m |= 1 << e
    return m


def dst(topo, d, core):
    rid, pid = topo.addr(d, core)
    return DstId(rid=rid, pnc=pid)


def slots(q):
    return LOW


def pos(q, k):
    return ([j for s in slots(q) for j, way in s] + [0]).index(k)


def id_block(T, q, k):
    return T.idl[:, pos(q, k) * L:(pos(q, k) + 1) * L]


def pieces(q, k):
    return [(0, H, "a"), (H, K, "b")] if k in [j for s in slots(q)[1:] for j, way in s if way != "out"] else [(0, K, "a")]


def engine_sets(T, topo, rank):
    c = T.cores[rank]
    every = topo.engines(c, [h for h in topo.cores_of(c) if h != c][0])
    out = topo.engines(c, T.cores[rank ^ 1])
    return every, out, [e for e in every if e not in out]


def plan(T, topo, rank):
    c = T.cores[rank]
    every, out, inner = engine_sets(T, topo, rank)

    def reach(h):
        return sum(topo.may_write(h, d) for d in T.cores if d != c)

    free = sorted((h for h in topo.cores_of(c) if h != c), key=reach)
    todo = sorted(((k, way) for s in slots(rank) for k, way in s if way != "out"),
                  key=lambda e: (topo.same_plane(c, T.cores[rank ^ e[0]]), e[1] == "far"))
    helper = {}
    others = [q for q in range(DIRECT_IDS, N) if q != rank]
    strict = [q for q in others if not topo.same_plane(c, T.cores[q])]
    for k, way in todo:
        if len(helper) == len(others):
            helper[k] = helper[slots(rank)[0][0][0]]
            continue
        fit = [h for h in free if (topo.die(h) == topo.die(c)) == (way == "near") and topo.may_write(h, T.cores[rank ^ k])]
        short = len(strict) > sum(reach(h) == N - 1 for h in helper.values())
        helper[k] = fit[-1] if short and way == "far" else fit[0]
        free.remove(helper[k])
    far, hs = {}, sorted(set(helper.values()), key=reach)
    for q in others:
        h = [h for h in hs if topo.may_write(h, T.cores[q])][0]
        hs.remove(h)
        far[h] = q
    ways = {}
    for s in slots(rank):
        for i, (k, way) in enumerate(s):
            if len(s) == 1:
                eng = out if way == "out" else every
            elif s[0][1] == "out":
                eng = out[i * len(out) // 2:(i + 1) * len(out) // 2]
            else:
                eng = out if i else inner
            h = helper.get(k)
            ways[k] = (h, eng, eng if h is None else topo.engines(h, T.cores[rank ^ k]))
    return [q for q in range(DIRECT_IDS) if q != rank], far, ways


def write(topo, core, cores, engines, sem, src, dsts):
    return RemoteDMATransfer(dst_ids=[dst(topo, c, core) for c in cores], dma_engine_mask=bits(engines),
                             remote_sem=sem, srcs=[src], dsts=dsts)


def helper_program(g, core, T, topo, rank):
    S = T.sem
    near, far, ways = plan(T, topo, rank)
    sent = 0
    if core in far:
        q = far[core]
        g.wait_ge(S.hid, len(engine_sets(T, topo, rank)[2]))
        eng = topo.engines(core, T.cores[q])
        g.remote_dma_fused([write(topo, core, [T.cores[q]], eng, S.ida, T.idd[:], [id_block(T, q, q ^ rank)])],
                           local_sem=S.sent)
        sent += len(eng)
    for k, (h, feed, eng) in ways.items():
        if h == core:
            o = pos(rank, k) * K
            for c0, c1, x in pieces(rank, k):
                g.wait_ge(S["hp%d" % k + x], len(feed))
                g.remote_dma_fused([write(topo, core, [T.cores[rank ^ k]], eng, S["pk_s%d" % rank + x],
                                          T.pk[:, o + c0:o + c1], [T.ld[:, rank * K + c0:rank * K + c1]])],
                                   local_sem=S.sent)
                sent += len(eng)
    if sent:
        g.wait_ge(S.sent, sent)


def rank_program(g, core, T, topo):
    rank = T.rank_of(core)
    if rank is None:
        for r in range(N):
            if core in topo.cores_of(T.cores[r]):
                helper_program(g, core, T, topo, r)
        return
    near, far, ways = plan(T, topo, rank)
    every, out, inner = engine_sets(T, topo, rank)
    S = T.sem
    V, P, A = g.vector, g.tensor, g.scalar
    copy = ActivationFunctionType.Copy
    mult, add = AluOpType.mult, AluOpType.add
    shr, band, eq = AluOpType.logical_shift_right, AluOpType.bitwise_and, AluOpType.is_equal

    g.sync.dma_start(T.idd[:], T.ids[:]).then_inc(S.ldd, 16)
    if rank == 0:
        for i in range(16):
            (g.sync, A)[i % 2].dma_start(T.tab[i:128:16, :], T.mat[i // 4:128:16, :]).then_inc(S.ldm, 16)
    else:
        g.sync.dma_start(T.tab[:], T.mat[:]).then_inc(S.ldm, 16)
    A.dma_start(T.hsi[:], T.hs[:]).then_inc(S.ldh, 16)
    A.dma_start(id_block(T, rank, 0), T.ids[:]).then_inc(S.ldi, 16)

    def ids_to(qs):
        return write(topo, core, [T.cores[q] for q in qs], out, S.ida, T.idd[:], [id_block(T, q, q ^ rank) for q in qs])

    g.iota(T.ip[:], [[0, 1]], 0, 1).then_inc(S.io_s, 1)
    g.iota(T.im[:], [[1, 32], [0, 4]], 0, 0, allow_small_or_imprecise_dtypes=True).then_inc(S.io_s, 1)
    g.wait_ge(S.ldd, 16)
    g.remote_dma_fused([ids_to(near[:FIRST_IDS])], local_sem=S.sent)
    g.remote_dma_fused([write(topo, core, list(far), inner, S.hid, T.idd[:], [T.idd[:] for h in far]),
                        ids_to(near[FIRST_IDS:])], local_sem=S.sent)
    sent = 2 * len(out) + len(inner)
    for i, s in enumerate(slots(rank)):
        parts = sorted(((k, piece) for k, way in s for piece in pieces(rank, k)), key=lambda p: p[1][2])
        together = len(s) == 1
        n = 1 if len(parts) % len(s) else len(s)
        for call in [parts[j:j + n] for j in range(0, len(parts), n)]:
            tr = []
            for k, (c0, c1, x) in call:
                h, eng, last = ways[k]
                g.wait_ge(S["gk%d" % k + x], 2 if together else 1)
                src = T.pk[:, pos(rank, k) * K + c0:pos(rank, k) * K + c1]
                if h is None:
                    tr.append(write(topo, core, [T.cores[rank ^ k]], eng, S["pk_s%d" % rank + x], src,
                                    [T.ld[:, rank * K + c0:rank * K + c1]]))
                else:
                    tr.append(write(topo, core, [h], eng, S["hp%d" % k + x], src, [src]))
                sent += len(eng)
            g.remote_dma_fused(tr, local_sem=S.sent)
    g.wait_ge(S.sent, sent)

    h = [0]

    def step(ins):
        ins.then_inc(S.h, 1)
        h[0] += 1

    def settle():
        V.wait_ge(S.h, h[0])

    V.wait_ge(S.io_s, 2)
    step(V.tensor_scalar(T.kk[:, 0:1], T.ip[:], 2, 28, shr, band))
    step(V.tensor_scalar(T.kk[:, 1:2], T.ip[:], 3, None, band))
    settle()
    step(V.tensor_tensor(T.key[:], T.kk[:, 0:1], T.kk[:, 1:2], add))
    settle()
    V.tensor_scalar(T.sf[:], T.im[:], T.key[:], None, eq).then_inc(S.cs, 1)
    V.tensor_scalar(T.s32[:], T.im[:, 0:128:4], T.key[:], None, eq).then_inc(S.cs, 1)

    V.wait_ge(S.ldh, 16)
    step(V.tensor_copy(T.hsf[:], T.hsi[:]))
    settle()
    V.wait_ge(S.ldi, 16)
    V.wait_ge(S.ida, len(out) * (N - 1))
    halves = [(slice(0, 4 * L), S.h0), (slice(4 * L, 8 * L), S.h1)]
    for c, sem in halves:
        V.tensor_scalar(T.t1[:, c], T.idl[:, c], T.hsf[:, 0:1], T.hsf[:, 1:2], mult, add).then_inc(sem, 1)
    for c, sem in halves:
        V.wait_ge(sem, 1)
        V.tensor_scalar(T.t2[:, c], T.t1[:, c], 2, D - 1, shr, band).then_inc(sem, 1)
    for c, sem in halves:
        V.wait_ge(sem, 2)
        V.tensor_copy(T.off[:, c], T.t2[:, c]).then_inc(sem, 1)
    seen = {0: set(), 1: set()}

    def gather(e, k, c0, c1, x):
        E = (V, A)[e]
        half = pos(rank, k) // 4
        if half not in seen[e]:
            E.wait_ge(halves[half][1], 3)
            if not seen[e]:
                E.wait_ge(S.ldm, 256 if rank == 0 else 16)
            seen[e].add(half)
        o0, o1 = pos(rank, k) * K + c0, pos(rank, k) * K + c1
        win = T.tab[:, 0:D].indirect(T.off[:, o0 // 16:o1 // 16])
        ins = V.tensor_copy(T.pk[:, o0:o1], win) if e == 0 else A.activation(T.pk[:, o0:o1], win, copy)
        ins.then_inc(S["gk%d" % k + x], 1)

    for i, s in enumerate(slots(rank)):
        if len(s) == 1:
            for c0, c1, x in pieces(rank, s[0][0]):
                gather(0, s[0][0], c0, (c0 + c1) // 2, x)
                gather(1, s[0][0], (c0 + c1) // 2, c1, x)
        else:
            for e in (0, 1):
                for piece in pieces(rank, s[e][0]):
                    gather(e, s[e][0], *piece)
    gather(1, 0, 0, K, "a")

    def arrived(q, b):
        for c0, c1, x in pieces(q, rank ^ q):
            if c0 == b * W and q == rank:
                V.wait_ge(S.gk0a, 1)
            elif c0 == b * W:
                V.wait_ge(S["pk_s%d" % q + x], len(plan(T, topo, q)[2][rank ^ q][2]))

    def pick(q, b):
        o = pos(rank, 0) * K if q == rank else q * K
        return (T.pk if q == rank else T.ld)[:, o + b * W:o + (b + 1) * W]

    ps = [T.ps0, T.ps1, T.ps2, T.ps3]
    vs = [S["v_s%d" % b] for b in range(NS)]
    ts = [S["t_s%d" % b] for b in range(NS)]
    outs = [S.o0, S.o1, S.o2]
    P.wait_ge(S.cs, 2)
    for q in range(1, N):
        for b in range(NS):
            arrived(q, b)
            pr = T.pr[:, b * W:(b + 1) * W]
            if q == 1:
                arrived(0, b)
            else:
                V.wait_ge(ts[b], q - 1)
            V.tensor_tensor(pr, pick(0, b) if q == 1 else ps[b][:, 0:W], pick(q, b), mult).then_inc(vs[b], 1)
            P.wait_ge(vs[b], q)
            if q < N - 1:
                P.matmul(ps[b][:, 0:W], T.sf[:], pr, True, True).then_inc(ts[b], 1)
            elif b == 1:
                P.matmul(ps[0][:, 0:32], T.pr[:, 0:H], T.s32[:], True, True).then_inc(outs[0], 1)
            elif b > 1:
                P.matmul(ps[b][0:32, 0:W], T.s32[:], pr, True, True).then_inc(outs[b - 1], 1)

    V.wait_ge(outs[0], 1)
    V.transpose(T.yt[:], ps[0][:, 0:32]).then_inc(S.ya, 1)
    for b, sem in ((2, S.yb), (3, S.yc)):
        V.wait_ge(outs[b - 1], 1)
        V.tensor_copy(T.yu[0:32, (b - 2) * W:(b - 1) * W], ps[b][0:32, 0:W]).then_inc(sem, 1)
    for Q, blocks, b, ready, done in ((g.sync, (0, 1), 2, S.yb, S.sta), (A, (2, 3), 3, S.yc, S.stb)):
        Q.wait_ge(S.ya, 1)
        for i in blocks:
            Q.dma_start(T.y[:, 32 * i:32 * (i + 1)], T.yt[32 * i:32 * (i + 1), :]).then_inc(done, 16)
        Q.wait_ge(ready, 1)
        Q.dma_start(T.y[:, b * W:(b + 1) * W], T.yu[0:32, (b - 2) * W:(b - 1) * W]).then_inc(done, 16)
        Q.wait_ge(done, 48)
